import numpy as np
import ml_dtypes


def mxq(x, axis, fmt="e4m3"):
    dtype, down = {"e4m3": (ml_dtypes.float8_e4m3fn, 7), "e5m2": (ml_dtypes.float8_e5m2, 14)}[fmt]
    v = np.moveaxis(np.asarray(x, np.float32).astype(ml_dtypes.bfloat16).astype(np.float64), axis, -1)
    blocks = v.reshape(v.shape[:-1] + (-1, 32))
    amax = np.abs(blocks).max(-1, keepdims=True)
    byte = np.maximum(np.where(amax > 0, np.frexp(amax)[1] - 1 + 127, 0) - down, 1)
    scale = np.exp2(byte - 127.0)
    codes = (blocks / scale).astype(np.float32).astype(dtype).astype(np.float64)
    return np.moveaxis((codes * scale).reshape(v.shape), -1, axis)


WIDE = False


def mx_kscale(k):
    if not WIDE:
        return np.ones(k)
    levels = np.array([10, -10, 5, -5, 0])
    if k % 512:
        return np.exp2(np.random.permutation(np.resize(levels, k // 32))).repeat(32)
    a = np.empty((k // 512, 16))
    for p in range(k // 512):
        a[p, :8] = np.random.permutation(np.resize(levels, 8))
        for g in range(8):
            far = levels[np.abs(levels - a[p, g]) >= 10]
            a[p, g + 8] = far[np.random.randint(len(far))]
    return np.exp2(a.ravel()).repeat(32)


def f64(x):
    return np.asarray(x).astype(np.float64)


def striped(idx):
    return np.tile(idx.reshape(-1, 16).T, (8, 1)).astype(np.uint16)


def unstriped(offs):
    return offs[:16].T.reshape(-1).astype(np.int64)


def striped8(idx):
    return np.concatenate([x.reshape(-1, 16).T for x in idx]).astype(np.uint16)


def runs(offs, k):
    lists = np.stack([offs[16 * r : 16 * r + 16].T.reshape(-1) for r in range(8)]).astype(np.int64)
    return lists[np.arange(k) % 512 // 64]


def pack_weight(w):
    k, n = w.shape
    w = f64(np.asarray(w, np.float32).astype(ml_dtypes.bfloat16)).reshape(k // 32, 32, n)
    amax = np.abs(w).max(1)
    byte = np.clip(np.where(amax > 0, np.frexp(amax)[1] - 1 + 127 - 7, 1), 1, 254)
    scaled = (w * np.exp2(127.0 - byte)[:, None, :]).reshape(k, n).astype(np.float32)
    words = np.ascontiguousarray(scaled.reshape(k // 512, 128, 4, n).transpose(0, 1, 3, 2)).astype(ml_dtypes.float8_e4m3fn).view(np.uint8)
    return words, np.ascontiguousarray(byte.astype(np.uint8).reshape(k // 512, 16, n))


def unpack_weight(words, scales):
    g, p, n, _ = words.shape
    vals = np.ascontiguousarray(words).view(ml_dtypes.float8_e4m3fn).astype(np.float64) * np.repeat(np.exp2(scales.astype(np.float64) - 127.0), 8, axis=1)[..., None]
    return vals.transpose(0, 1, 3, 2).reshape(g * 512, n)


def sigmoid(v):
    return 1.0 / (1.0 + np.exp(-np.maximum(v, -700.0)))


K, T, S, G, H, W = 512, 1024, 512, 2048, 512, 1024


def setup_inputs():
    n = np.random.standard_normal
    s = mx_kscale(K)[:, None]
    packed_xT = pack_weight(n((K, T)) * s)
    packed_dT = pack_weight(n((K, G)) / s)
    return {
        "x_words": packed_xT[0],
        "x_scales": packed_xT[1],
        "d_words": packed_dT[0],
        "d_scales": packed_dT[1],
        "gs": (np.random.uniform(0.5, 1.5, (K, 1)) * s).astype(np.float32),
        "sl": np.random.uniform(1.0, 2.0, (H, 1)).astype(np.float32),
        "th": (0.5 * n((H, 1))).astype(np.float32),
        "sl2": np.random.uniform(1.0, 2.0, (H, 1)).astype(np.float32),
        "th2": (0.5 * n((H, 1))).astype(np.float32),
        "offs": striped(np.random.permutation(T)[:S]),
        "k1": striped8(np.random.randint(0, G, (8, H))),
        "n1": striped(np.random.randint(0, S, W)),
        "n2": striped(np.random.permutation(S)),
        "k2": striped8(np.random.randint(0, G, (8, H))),
        "n3": striped8(np.stack([np.random.permutation(S) for _ in range(8)])),
        "n4": striped8(np.stack([np.random.permutation(S) for _ in range(8)])),
    }


def reference(x_words, x_scales, d_words, d_scales, gs, sl, th, sl2, th2, offs, k1, n1, n2, k2, n3, n4):
    d_k2 = unpack_weight(d_words, d_scales)[np.arange(K)[:, None], runs(k2, K)]
    d_k1 = unpack_weight(d_words, d_scales)[np.arange(K)[:, None], runs(k1, K)]
    xq = unpack_weight(x_words, x_scales)[:, unstriped(offs)]
    h = 0.0625 * (d_k1.T @ xq)
    mb = h[:, unstriped(n1)]
    mx = mb.reshape(H, S, 2).max(axis=2)
    st = h - mx
    z = f64(gs) * (np.maximum(st, st[:, unstriped(n2)]))
    h2 = 0.0625 * ((d_k2.T @ mxq(z, 0, "e4m3")))
    sg = sigmoid(f64(sl) * (h2[np.arange(H)[:, None], runs(n3, H)] - f64(th)))
    sg2 = sigmoid(f64(sl2) * (f64(th2) - (h2[np.arange(H)[:, None], runs(n4, H)])))
    return 2.0 * ((h2 * sg) * sg2)

@@ -1,0 +1,250 @@
+from contextlib import ExitStack
+
+import concourse.mybir as mybir
+
+K, T, S, G, H, W = 512, 1024, 512, 2048, 512, 1024
+FLOPS = 2 * K * H * S * 2
+
+F32 = mybir.dt.float32
+BF16 = mybir.dt.bfloat16
+I32 = mybir.dt.int32
+U32 = mybir.dt.uint32
+U16 = mybir.dt.uint16
+U8 = mybir.dt.uint8
+FP8X4 = mybir.dt.float8_e4m3fn_x4
+ALU = mybir.AluOpType
+ACT = mybir.ActivationFunctionType
+
+P = 128
+PACK = 4
+SPARE = 32
+
+
+def tile_picked_codeghopmecr_none_p_kernel(
+    tc, x_words, x_scales, d_words, d_scales, gs, sl, th, sl2, th2, offs, k1, n1, n2, k2, n3, n4, out
+):
+    nc = tc.nc
+    with ExitStack() as ctx:
+        sb = ctx.enter_context(tc.tile_pool(name="sb", bufs=1))
+        psum = ctx.enter_context(tc.psum_pool(name="psum", bufs=1))
+
+        def load_list(name, src):
+            tile = sb.tile(list(src.shape), U16, name=name)
+            nc.sync.dma_start(tile[:], src)
+            return tile
+
+        def cleared(name, width):
+            tile = sb.tile([P, width], U8, name=name, align_bytes=64)
+            nc.gpsimd.memset(tile[:].bitcast(I32), 0)
+            return tile
+
+        def load_words(name, src, width, queue):
+            tile = sb.tile([P, width], U32, name=name, align_bytes=64)
+            queue.dma_start(tile[:].bitcast(I32), src[0].rearrange("p n t -> p (n t)").bitcast(I32))
+            return tile
+
+        def load_vec(name, src):
+            tile = sb.tile([P, PACK], F32, name=name)
+            nc.gpsimd.dma_start(tile[:], src.rearrange("(p t) o -> p (t o)", t=PACK))
+            return tile
+
+        def gather(name, dtype, table, offsets, tag):
+            tile = sb.tile([P, 512], dtype, name=name, tag=tag, align_bytes=64)
+            nc.vector.tensor_copy(tile[:], table[:].indirect(offsets[:]))
+            return tile
+
+        def deal(dst, src, run):
+            nc.vector.tensor_copy(
+                dst.rearrange("p (t c i) -> p c t i", t=PACK, i=run),
+                src.rearrange("p (c i t) -> p c t i", t=PACK, i=run),
+            )
+
+        def place_odd_rows(plane, queue):
+            words = plane[:].bitcast(I32)
+            for r in range(2):
+                queue.dma_start(words[2 + r : P : 32, :], words[16 + r : P : 32, :])
+
+        d_sc = cleared("d_sc", G)
+        x_sc = cleared("x_sc", T)
+        offs_t = load_list("offs_t", offs)
+        x_w = load_words("x_w", x_words, T, nc.sync)
+        k1_t = load_list("k1_t", k1)
+        for r in range(2):
+            nc.sync.dma_start(d_sc[:].bitcast(I32)[r:P:16, :], d_scales[0].bitcast(I32)[r:16:2, :])
+        d_w = load_words("d_w", d_words, G, nc.sync)
+        for q in range(4):
+            nc.sync.dma_start(
+                x_sc[:].bitcast(I32)[32 * q : 32 * q + 4, :], x_scales[0].bitcast(I32)[4 * q : 4 * q + 4, :]
+            )
+
+        plane1 = sb.tile([P, H], U8, name="plane1", align_bytes=64)
+        d1_sc = gather("d1_sc", U8, d_sc, k1_t, "d1_sc")
+        deal(plane1[:], d1_sc[:], 16)
+        place_odd_rows(plane1, nc.sync)
+        xg_w = gather("xg_w", U32, x_w, offs_t, "d1_sc")
+        d1_w = gather("d1_w", U32, d_w, k1_t, "d1_w")
+        w1 = sb.tile([P, H], U32, name="w1", align_bytes=64)
+        deal(w1[:], d1_w[:], 4)
+        xg_sc = gather("xg_sc", U8, x_sc, offs_t, "xg_sc")
+
+        n1_t = load_list("n1_t", n1)
+        k2_t = load_list("k2_t", k2)
+        n2_t = load_list("n2_t", n2)
+        n3_t = load_list("n3_t", n3)
+        n4_t = load_list("n4_t", n4)
+        sl_t = load_vec("sl_t", sl)
+        th_t = load_vec("th_t", th)
+        sl2_t = load_vec("sl2_t", sl2)
+        th2_t = load_vec("th2_t", th2)
+        gs_t = load_vec("gs_t", gs)
+
+        bias1 = sb.tile([P, PACK], F32, name="bias1")
+        minus_sl = sb.tile([P, PACK], F32, name="minus_sl")
+        scale2 = sb.tile([P, PACK], F32, name="scale2")
+        bias2 = sb.tile([P, PACK], F32, name="bias2")
+        nc.scalar.activation(minus_sl[:], sl_t[:], ACT.Copy, scale=-1.0)
+        nc.scalar.activation(scale2[:], sl2_t[:], ACT.Copy, scale=-1.0)
+        for t in range(PACK):
+            col = slice(t, t + 1)
+            nc.scalar.activation(bias1[:, col], th_t[:, col], ACT.Copy, scale=minus_sl[:, col])
+            nc.scalar.activation(bias2[:, col], th2_t[:, col], ACT.Copy, scale=sl2_t[:, col])
+
+        banks = [psum.tile([P, S], F32, name="bank%d" % b) for b in range(2 * PACK)]
+        for t in range(PACK):
+            cols = slice(t * P, (t + 1) * P)
+            nc.tensor.matmul_mx(
+                out=banks[t][:],
+                lhsT=w1[:, cols].bitcast(FP8X4),
+                lhsT_scale=plane1[:, cols],
+                rhs=xg_w[:].bitcast(FP8X4),
+                rhs_scale=xg_sc[:],
+                start=True,
+                stop=True,
+            )
+
+        plane2 = sb.tile([P, H], U8, name="plane2", align_bytes=64)
+        d2_sc = gather("d2_sc", U8, d_sc, k2_t, "d1_w")
+        deal(plane2[:], d2_sc[:], 16)
+        place_odd_rows(plane2, nc.sync)
+
+        h = [sb.tile([P, S + SPARE], F32, name="h%d" % t) for t in range(PACK)]
+        mb = [sb.tile([P, W], F32, name="mb%d" % t) for t in range(PACK)]
+        st = [sb.tile([P, S + SPARE], F32, name="st%d" % t) for t in range(PACK)]
+        mx = [sb.tile([P, S], F32, name="mx%d" % t, tag="mx%d" % t, align_bytes=64) for t in range(PACK)]
+        stn = [sb.tile([P, S], F32, name="stn%d" % t) for t in range(PACK)]
+        big = [sb.tile([P, S], F32, name="big%d" % t) for t in range(PACK)]
+        zpair = sb.tile([P, 2, 2, S // 2, 2], BF16, name="zpair", align_bytes=64)
+        z = sb.tile([P, S * PACK], BF16, name="z", align_bytes=64)
+
+        def evac(t):
+            nc.scalar.activation(h[t][:, 0:S], banks[t][:], ACT.Copy, scale=0.0625)
+
+        def members(t, half, on_vector):
+            window = h[t][:].indirect(n1_t[:, half * 32 : (half + 1) * 32])
+            dst = mb[t][:, half * S : (half + 1) * S]
+            if on_vector:
+                nc.vector.tensor_copy(dst, window)
+            else:
+                nc.scalar.activation(dst, window, ACT.Copy)
+
+        def stand(t):
+            pairs = mb[t][:].rearrange("p (j e) -> p e j", e=2)
+            nc.vector.tensor_tensor(mx[t][:], pairs[:, 0, :], pairs[:, 1, :], ALU.max)
+            nc.vector.tensor_tensor(st[t][:, 0:S], h[t][:, 0:S], mx[t][:], ALU.subtract)
+
+        halves = [slice(0, S // 2), slice(S // 2, S)]
+        whole = slice(0, S)
+
+        def neighbour(t, cols, on_vector):
+            window = st[t][:].indirect(n2_t[:, cols.start // 16 : cols.stop // 16])
+            if on_vector:
+                nc.vector.tensor_copy(stn[t][:, cols], window)
+            else:
+                nc.scalar.activation(stn[t][:, cols], window, ACT.Copy)
+
+        def weigh(t, cols):
+            nc.vector.tensor_tensor(big[t][:, cols], st[t][:, cols], stn[t][:, cols], ALU.max)
+            nc.vector.tensor_scalar(
+                zpair[:, 2 * cols.start // S : 2 * cols.stop // S, t // 2, :, t % 2],
+                big[t][:, cols].rearrange("p (a j) -> p a j", j=S // 2),
+                gs_t[:, t : t + 1],
+                None,
+                ALU.mult,
+            )
+
+        z_w = sb.tile([P, S], U32, name="z_w", align_bytes=64)
+        z_sc = sb.tile([P, S], U8, name="z_sc", align_bytes=64)
+        z_words = z[:].bitcast(F32).rearrange("p (j u) -> p j u", u=2)
+
+        def quantise(cols):
+            pair_words = zpair[:, 2 * cols.start // S].rearrange("p u j e -> p u (j e)").bitcast(F32)
+            nc.vector.tensor_copy(z_words[:, cols, :], pair_words.rearrange("p u j -> p j u"))
+            nc.vector.quantize_mx(
+                out=z_w[:, cols].bitcast(FP8X4), scales=z_sc[:, cols], in_=z[:, PACK * cols.start : PACK * cols.stop]
+            )
+
+        evac(0)
+        members(0, 0, False)
+        members(0, 1, True)
+        evac(1)
+        stand(0)
+        members(1, 0, False)
+        members(1, 1, True)
+        evac(2)
+        stand(1)
+        members(2, 0, False)
+        members(2, 1, False)
+        d2_w = gather("d2_w", U32, d_w, k2_t, "mx1")
+        w2 = sb.tile([P, H], U32, name="w2", align_bytes=64)
+        deal(w2[:], d2_w[:], 4)
+        evac(3)
+        stand(2)
+        members(3, 0, False)
+        members(3, 1, False)
+        for cols in halves:
+            neighbour(0, cols, True)
+        weigh(0, whole)
+        neighbour(1, whole, False)
+        stand(3)
+        neighbour(2, whole, False)
+        for cols in halves:
+            neighbour(3, cols, False)
+        weigh(1, whole)
+        weigh(2, whole)
+        for cols in halves:
+            weigh(3, cols)
+            quantise(cols)
+
+        out_rows = out.rearrange("(p t) c -> p t c", t=PACK)
+        for t in range(PACK):
+            rows = slice(t * P, (t + 1) * P)
+            for cols in halves:
+                nc.tensor.matmul_mx(
+                    out=banks[PACK + t][:, cols],
+                    lhsT=w2[:, rows].bitcast(FP8X4),
+                    lhsT_scale=plane2[:, rows],
+                    rhs=z_w[:, cols].bitcast(FP8X4),
+                    rhs_scale=z_sc[:, cols],
+                    start=True,
+                    stop=True,
+                )
+        for t in range(PACK):
+            nc.vector.tensor_scalar(mb[t][:, 0:S], banks[PACK + t][:], 0.0625, None, ALU.mult)
+        for t in range(PACK):
+            col = slice(t, t + 1)
+            sg = sb.tile([P, S], F32, name="sg%d" % t)
+            sg2 = sb.tile([P, S], F32, name="sg2_%d" % t)
+            part = sb.tile([P, S], F32, name="part%d" % t)
+            res = sb.tile([P, S], F32, name="res%d" % t)
+            nc.scalar.activation(sg[:], mb[t][:].indirect(n3_t[:]), ACT.Sigmoid, bias=bias1[:, col], scale=sl_t[:, col])
+            nc.vector.scalar_tensor_tensor(part[:], mb[t][:, 0:S], 2.0, sg[:], ALU.mult, ALU.mult)
+            for cols in halves if t == PACK - 1 else [slice(0, S)]:
+                nc.scalar.activation(
+                    sg2[:, cols],
+                    mb[t][:].indirect(n4_t[:, cols.start // 16 : cols.stop // 16]),
+                    ACT.Sigmoid,
+                    bias=bias2[:, col],
+                    scale=scale2[:, col],
+                )
+                nc.vector.tensor_tensor(res[:, cols], part[:, cols], sg2[:, cols], ALU.mult)
+                nc.sync.dma_start(out_rows[:, t, cols], res[:, cols])

@@ -45,7 +45,7 @@ def tile_picked_codeghopmecr_none_p_kernel(
 
         def load_vec(name, src):
             tile = sb.tile([P, PACK], F32, name=name)
-            nc.gpsimd.dma_start(tile[:], src.rearrange("(p t) o -> p (t o)", t=PACK))
+            nc.sync.dma_start(tile[:], src.rearrange("(p t) o -> p (t o)", t=PACK))
             return tile
 
         def gather(name, dtype, table, offsets, tag):
@@ -66,68 +66,81 @@ def tile_picked_codeghopmecr_none_p_kernel(
 
         d_sc = cleared("d_sc", G)
         x_sc = cleared("x_sc", T)
-        offs_t = load_list("offs_t", offs)
-        x_w = load_words("x_w", x_words, T, nc.sync)
         k1_t = load_list("k1_t", k1)
         for r in range(2):
             nc.sync.dma_start(d_sc[:].bitcast(I32)[r:P:16, :], d_scales[0].bitcast(I32)[r:16:2, :])
-        d_w = load_words("d_w", d_words, G, nc.sync)
+        offs_t = load_list("offs_t", offs)
         for q in range(4):
             nc.sync.dma_start(
                 x_sc[:].bitcast(I32)[32 * q : 32 * q + 4, :], x_scales[0].bitcast(I32)[4 * q : 4 * q + 4, :]
             )
+        d_w = load_words("d_w", d_words, G, nc.sync)
+        x_w = load_words("x_w", x_words, T, nc.sync)
+
+        halves = [slice(0, S // 2), slice(S // 2, S)]
+        whole = slice(0, S)
 
         plane1 = sb.tile([P, H], U8, name="plane1", align_bytes=64)
         d1_sc = gather("d1_sc", U8, d_sc, k1_t, "d1_sc")
         deal(plane1[:], d1_sc[:], 16)
         place_odd_rows(plane1, nc.sync)
-        xg_w = gather("xg_w", U32, x_w, offs_t, "d1_sc")
+        xg_sc = gather("xg_sc", U8, x_sc, offs_t, "xg_sc")
         d1_w = gather("d1_w", U32, d_w, k1_t, "d1_w")
         w1 = sb.tile([P, H], U32, name="w1", align_bytes=64)
         deal(w1[:], d1_w[:], 4)
-        xg_sc = gather("xg_sc", U8, x_sc, offs_t, "xg_sc")
+        xg_w = sb.tile([P, S], U32, name="xg_w", align_bytes=64)
+        for cols in halves:
+            nc.vector.tensor_copy(xg_w[:, cols], x_w[:].indirect(offs_t[:, cols.start // 16 : cols.stop // 16]))
 
-        n1_t = load_list("n1_t", n1)
         k2_t = load_list("k2_t", k2)
+        n1_t = load_list("n1_t", n1)
         n2_t = load_list("n2_t", n2)
         n3_t = load_list("n3_t", n3)
         n4_t = load_list("n4_t", n4)
-        sl_t = load_vec("sl_t", sl)
+        slopes = sb.tile([P, 2, 2 * PACK], F32, name="slopes")
+        for i, src in enumerate((sl, sl2)):
+            nc.sync.dma_start(slopes[:, i, 0:PACK], src.rearrange("(p t) o -> p (t o)", t=PACK))
         th_t = load_vec("th_t", th)
-        sl2_t = load_vec("sl2_t", sl2)
         th2_t = load_vec("th2_t", th2)
         gs_t = load_vec("gs_t", gs)
 
+        minus = sb.tile([P, 2, PACK], F32, name="minus")
         bias1 = sb.tile([P, PACK], F32, name="bias1")
-        minus_sl = sb.tile([P, PACK], F32, name="minus_sl")
-        scale2 = sb.tile([P, PACK], F32, name="scale2")
         bias2 = sb.tile([P, PACK], F32, name="bias2")
-        nc.scalar.activation(minus_sl[:], sl_t[:], ACT.Copy, scale=-1.0)
-        nc.scalar.activation(scale2[:], sl2_t[:], ACT.Copy, scale=-1.0)
-        for t in range(PACK):
-            col = slice(t, t + 1)
-            nc.scalar.activation(bias1[:, col], th_t[:, col], ACT.Copy, scale=minus_sl[:, col])
-            nc.scalar.activation(bias2[:, col], th2_t[:, col], ACT.Copy, scale=sl2_t[:, col])
+        gain = sb.tile([P, PACK], F32, name="gain")
+        nc.scalar.activation(minus[:], slopes[:, :, 0:PACK], ACT.Copy, scale=-1.0)
+        nc.gpsimd.tensor_tensor(bias1[:], minus[:, 0, :], th_t[:], ALU.mult)
+        nc.gpsimd.tensor_tensor(bias2[:], slopes[:, 1, 0:PACK], th2_t[:], ALU.mult)
+        nc.gpsimd.tensor_scalar(gain[:], gs_t[:], 0.0625, 0.0, ALU.mult, ALU.add)
 
         banks = [psum.tile([P, S], F32, name="bank%d" % b) for b in range(2 * PACK)]
-        for t in range(PACK):
-            cols = slice(t * P, (t + 1) * P)
+        h = [sb.tile([P, S + SPARE], F32, name="h%d" % t) for t in range(PACK)]
+        early = [(0, halves[0], PACK), (1, halves[0], PACK + 1)]
+        late = [(0, halves[1], 0), (1, halves[1], 1), (2, whole, 2), (3, whole, 3)]
+        for t, cols, bank in early + late:
+            rows = slice(t * P, (t + 1) * P)
             nc.tensor.matmul_mx(
-                out=banks[t][:],
-                lhsT=w1[:, cols].bitcast(FP8X4),
-                lhsT_scale=plane1[:, cols],
-                rhs=xg_w[:].bitcast(FP8X4),
-                rhs_scale=xg_sc[:],
+                out=banks[bank][:, cols],
+                lhsT=w1[:, rows].bitcast(FP8X4),
+                lhsT_scale=plane1[:, rows],
+                rhs=xg_w[:, cols].bitcast(FP8X4),
+                rhs_scale=xg_sc[:, cols],
                 start=True,
                 stop=True,
             )
 
+        def evac(piece):
+            t, cols, bank = piece
+            nc.scalar.activation(h[t][:, cols], banks[bank][:, cols], ACT.Copy)
+
+        for piece in early:
+            evac(piece)
+
         plane2 = sb.tile([P, H], U8, name="plane2", align_bytes=64)
-        d2_sc = gather("d2_sc", U8, d_sc, k2_t, "d1_w")
+        d2_sc = gather("d2_sc", U8, d_sc, k2_t, "d2_sc")
         deal(plane2[:], d2_sc[:], 16)
         place_odd_rows(plane2, nc.sync)
 
-        h = [sb.tile([P, S + SPARE], F32, name="h%d" % t) for t in range(PACK)]
         mb = [sb.tile([P, W], F32, name="mb%d" % t) for t in range(PACK)]
         st = [sb.tile([P, S + SPARE], F32, name="st%d" % t) for t in range(PACK)]
         mx = [sb.tile([P, S], F32, name="mx%d" % t, tag="mx%d" % t, align_bytes=64) for t in range(PACK)]
@@ -135,9 +148,6 @@ def tile_picked_codeghopmecr_none_p_kernel(
         big = [sb.tile([P, S], F32, name="big%d" % t) for t in range(PACK)]
         zpair = sb.tile([P, 2, 2, S // 2, 2], BF16, name="zpair", align_bytes=64)
         z = sb.tile([P, S * PACK], BF16, name="z", align_bytes=64)
-
-        def evac(t):
-            nc.scalar.activation(h[t][:, 0:S], banks[t][:], ACT.Copy, scale=0.0625)
 
         def members(t, half, on_vector):
             window = h[t][:].indirect(n1_t[:, half * 32 : (half + 1) * 32])
@@ -152,9 +162,6 @@ def tile_picked_codeghopmecr_none_p_kernel(
             nc.vector.tensor_tensor(mx[t][:], pairs[:, 0, :], pairs[:, 1, :], ALU.max)
             nc.vector.tensor_tensor(st[t][:, 0:S], h[t][:, 0:S], mx[t][:], ALU.subtract)
 
-        halves = [slice(0, S // 2), slice(S // 2, S)]
-        whole = slice(0, S)
-
         def neighbour(t, cols, on_vector):
             window = st[t][:].indirect(n2_t[:, cols.start // 16 : cols.stop // 16])
             if on_vector:
@@ -167,7 +174,7 @@ def tile_picked_codeghopmecr_none_p_kernel(
             nc.vector.tensor_scalar(
                 zpair[:, 2 * cols.start // S : 2 * cols.stop // S, t // 2, :, t % 2],
                 big[t][:, cols].rearrange("p (a j) -> p a j", j=S // 2),
-                gs_t[:, t : t + 1],
+                gain[:, t : t + 1],
                 None,
                 ALU.mult,
             )
@@ -183,29 +190,29 @@ def tile_picked_codeghopmecr_none_p_kernel(
                 out=z_w[:, cols].bitcast(FP8X4), scales=z_sc[:, cols], in_=z[:, PACK * cols.start : PACK * cols.stop]
             )
 
-        evac(0)
+        evac(late[0])
         members(0, 0, False)
         members(0, 1, True)
-        evac(1)
+        evac(late[1])
         stand(0)
         members(1, 0, False)
         members(1, 1, True)
-        evac(2)
+        evac(late[2])
         stand(1)
         members(2, 0, False)
         members(2, 1, False)
-        d2_w = gather("d2_w", U32, d_w, k2_t, "mx1")
+        d2_w = gather("d2_w", U32, d_w, k2_t, "mx0")
         w2 = sb.tile([P, H], U32, name="w2", align_bytes=64)
         deal(w2[:], d2_w[:], 4)
-        evac(3)
+        evac(late[3])
         stand(2)
         members(3, 0, False)
         members(3, 1, False)
-        for cols in halves:
-            neighbour(0, cols, True)
+        stand(3)
+        neighbour(0, halves[0], True)
+        neighbour(0, halves[1], False)
         weigh(0, whole)
         neighbour(1, whole, False)
-        stand(3)
         neighbour(2, whole, False)
         for cols in halves:
             neighbour(3, cols, False)
@@ -216,27 +223,27 @@ def tile_picked_codeghopmecr_none_p_kernel(
             quantise(cols)
 
         out_rows = out.rearrange("(p t) c -> p t c", t=PACK)
-        for t in range(PACK):
+        pieces = [(0, halves[0], PACK), (0, halves[1], 0)] + [(t, whole, PACK + t) for t in range(1, PACK)]
+        for t, cols, bank in pieces:
             rows = slice(t * P, (t + 1) * P)
-            for cols in halves:
-                nc.tensor.matmul_mx(
-                    out=banks[PACK + t][:, cols],
-                    lhsT=w2[:, rows].bitcast(FP8X4),
-                    lhsT_scale=plane2[:, rows],
-                    rhs=z_w[:, cols].bitcast(FP8X4),
-                    rhs_scale=z_sc[:, cols],
-                    start=True,
-                    stop=True,
-                )
-        for t in range(PACK):
-            nc.vector.tensor_scalar(mb[t][:, 0:S], banks[PACK + t][:], 0.0625, None, ALU.mult)
+            nc.tensor.matmul_mx(
+                out=banks[bank][:, cols],
+                lhsT=w2[:, rows].bitcast(FP8X4),
+                lhsT_scale=plane2[:, rows],
+                rhs=z_w[:, cols].bitcast(FP8X4),
+                rhs_scale=z_sc[:, cols],
+                start=True,
+                stop=True,
+            )
+        for t, cols, bank in pieces:
+            nc.vector.tensor_scalar(mb[t][:, cols], banks[bank][:, cols], 0.0625, None, ALU.mult)
         for t in range(PACK):
             col = slice(t, t + 1)
             sg = sb.tile([P, S], F32, name="sg%d" % t)
             sg2 = sb.tile([P, S], F32, name="sg2_%d" % t)
-            part = sb.tile([P, S], F32, name="part%d" % t)
+            part = sb.tile([P, S], F32, name="part%d" % t, tag="part")
             res = sb.tile([P, S], F32, name="res%d" % t)
-            nc.scalar.activation(sg[:], mb[t][:].indirect(n3_t[:]), ACT.Sigmoid, bias=bias1[:, col], scale=sl_t[:, col])
+            nc.scalar.activation(sg[:], mb[t][:].indirect(n3_t[:]), ACT.Sigmoid, bias=bias1[:, col], scale=slopes[:, 0, col])
             nc.vector.scalar_tensor_tensor(part[:], mb[t][:, 0:S], 2.0, sg[:], ALU.mult, ALU.mult)
             for cols in halves if t == PACK - 1 else [slice(0, S)]:
                 nc.scalar.activation(
@@ -244,7 +251,7 @@ def tile_picked_codeghopmecr_none_p_kernel(
                     mb[t][:].indirect(n4_t[:, cols.start // 16 : cols.stop // 16]),
                     ACT.Sigmoid,
                     bias=bias2[:, col],
-                    scale=scale2[:, col],
+                    scale=minus[:, 1, col],
                 )
                 nc.vector.tensor_tensor(res[:, cols], part[:, cols], sg2[:, cols], ALU.mult)
                 nc.sync.dma_start(out_rows[:, t, cols], res[:, cols])

@@ -35,7 +35,7 @@ def tile_picked_codeghopmecr_none_p_kernel(
 
         def cleared(name, width):
             tile = sb.tile([P, width], U8, name=name, align_bytes=64)
-            nc.gpsimd.memset(tile[:].bitcast(I32), 0)
+            nc.vector.memset(tile[:].bitcast(I32), 0)
             return tile
 
         def load_words(name, src, width, queue):
@@ -48,28 +48,37 @@ def tile_picked_codeghopmecr_none_p_kernel(
             nc.sync.dma_start(tile[:], src.rearrange("(p t) o -> p (t o)", t=PACK))
             return tile
 
-        def gather(name, dtype, table, offsets, tag):
-            tile = sb.tile([P, 512], dtype, name=name, tag=tag, align_bytes=64)
-            nc.vector.tensor_copy(tile[:], table[:].indirect(offsets[:]))
-            return tile
+        halves = [slice(0, S // 2), slice(S // 2, S)]
+        whole = slice(0, S)
 
-        def deal(dst, src, run):
-            nc.vector.tensor_copy(
-                dst.rearrange("p (t c i) -> p c t i", t=PACK, i=run),
-                src.rearrange("p (c i t) -> p c t i", t=PACK, i=run),
-            )
+        def entries(offsets, cols):
+            return offsets[:, cols.start // 16 : cols.stop // 16]
+
+        def pick_and_deal(name, dtype, table, offsets, tag, pieces):
+            run = 16 if dtype == U8 else 4
+            picked = sb.tile([P, H], dtype, name=name + "_picked", tag=tag, align_bytes=64)
+            dealt = sb.tile([P, H], dtype, name=name, align_bytes=64)
+            for cols in pieces:
+                nc.vector.tensor_copy(picked[:, cols], table[:].indirect(entries(offsets, cols)))
+            for cols in pieces:
+                nc.vector.tensor_copy(
+                    dealt[:]
+                    .rearrange("p (t m) -> p t m", t=PACK)[:, :, cols.start // PACK : cols.stop // PACK]
+                    .rearrange("p t (c i) -> p c t i", i=run),
+                    picked[:, cols].rearrange("p (c i t) -> p c t i", t=PACK, i=run),
+                )
+            return dealt
 
         def place_odd_rows(plane, queue):
             words = plane[:].bitcast(I32)
-            for r in range(2):
-                queue.dma_start(words[2 + r : P : 32, :], words[16 + r : P : 32, :])
+            for r in range(1, 4):
+                queue.dma_start(words[r:P:32, :], words[8 * r : P : 32, :])
 
         d_sc = cleared("d_sc", G)
         x_sc = cleared("x_sc", T)
         k1_t = load_list("k1_t", k1)
-        for r in range(2):
-            nc.sync.dma_start(d_sc[:].bitcast(I32)[r:P:16, :], d_scales[0].bitcast(I32)[r:16:2, :])
         offs_t = load_list("offs_t", offs)
+        nc.sync.dma_start(d_sc[:].bitcast(I32)[0:P:8, :], d_scales[0].bitcast(I32))
         for q in range(4):
             nc.sync.dma_start(
                 x_sc[:].bitcast(I32)[32 * q : 32 * q + 4, :], x_scales[0].bitcast(I32)[4 * q : 4 * q + 4, :]
@@ -77,17 +86,11 @@ def tile_picked_codeghopmecr_none_p_kernel(
         d_w = load_words("d_w", d_words, G, nc.sync)
         x_w = load_words("x_w", x_words, T, nc.sync)
 
-        halves = [slice(0, S // 2), slice(S // 2, S)]
-        whole = slice(0, S)
-
-        plane1 = sb.tile([P, H], U8, name="plane1", align_bytes=64)
-        d1_sc = gather("d1_sc", U8, d_sc, k1_t, "d1_sc")
-        deal(plane1[:], d1_sc[:], 16)
+        plane1 = pick_and_deal("plane1", U8, d_sc, k1_t, "d1_sc", halves)
         place_odd_rows(plane1, nc.sync)
-        xg_sc = gather("xg_sc", U8, x_sc, offs_t, "xg_sc")
-        d1_w = gather("d1_w", U32, d_w, k1_t, "d1_w")
-        w1 = sb.tile([P, H], U32, name="w1", align_bytes=64)
-        deal(w1[:], d1_w[:], 4)
+        xg_sc = sb.tile([P, S], U8, name="xg_sc", align_bytes=64)
+        nc.vector.tensor_copy(xg_sc[:], x_sc[:].indirect(offs_t[:]))
+        w1 = pick_and_deal("w1", U32, d_w, k1_t, "d1_w", halves)
         xg_w = sb.tile([P, S], U32, name="xg_w", align_bytes=64)
         for cols in halves:
             nc.vector.tensor_copy(xg_w[:, cols], x_w[:].indirect(offs_t[:, cols.start // 16 : cols.stop // 16]))
@@ -136,9 +139,7 @@ def tile_picked_codeghopmecr_none_p_kernel(
         for piece in early:
             evac(piece)
 
-        plane2 = sb.tile([P, H], U8, name="plane2", align_bytes=64)
-        d2_sc = gather("d2_sc", U8, d_sc, k2_t, "d2_sc")
-        deal(plane2[:], d2_sc[:], 16)
+        plane2 = pick_and_deal("plane2", U8, d_sc, k2_t, "d2_sc", halves)
         place_odd_rows(plane2, nc.sync)
 
         mb = [sb.tile([P, W], F32, name="mb%d" % t) for t in range(PACK)]
@@ -201,9 +202,7 @@ def tile_picked_codeghopmecr_none_p_kernel(
         stand(1)
         members(2, 0, False)
         members(2, 1, False)
-        d2_w = gather("d2_w", U32, d_w, k2_t, "mx0")
-        w2 = sb.tile([P, H], U32, name="w2", align_bytes=64)
-        deal(w2[:], d2_w[:], 4)
+        w2 = pick_and_deal("w2", U32, d_w, k2_t, "mx0", [whole])
         evac(late[3])
         stand(2)
         members(3, 0, False)
@@ -235,20 +234,29 @@ def tile_picked_codeghopmecr_none_p_kernel(
                 start=True,
                 stop=True,
             )
+        last = PACK - 1
+        h2 = mb[:last] + [mx[last]]
         for t, cols, bank in pieces:
-            nc.vector.tensor_scalar(mb[t][:, cols], banks[bank][:, cols], 0.0625, None, ALU.mult)
+            nc.vector.tensor_scalar(h2[t][:, cols], banks[bank][:, cols], 0.0625, None, ALU.mult)
         for t in range(PACK):
             col = slice(t, t + 1)
             sg = sb.tile([P, S], F32, name="sg%d" % t)
             sg2 = sb.tile([P, S], F32, name="sg2_%d" % t)
             part = sb.tile([P, S], F32, name="part%d" % t, tag="part")
             res = sb.tile([P, S], F32, name="res%d" % t)
-            nc.scalar.activation(sg[:], mb[t][:].indirect(n3_t[:]), ACT.Sigmoid, bias=bias1[:, col], scale=slopes[:, 0, col])
-            nc.vector.scalar_tensor_tensor(part[:], mb[t][:, 0:S], 2.0, sg[:], ALU.mult, ALU.mult)
-            for cols in halves if t == PACK - 1 else [slice(0, S)]:
+            for cols in halves if t == last else [whole]:
+                nc.scalar.activation(
+                    sg[:, cols],
+                    h2[t][:].indirect(entries(n3_t, cols)),
+                    ACT.Sigmoid,
+                    bias=bias1[:, col],
+                    scale=slopes[:, 0, col],
+                )
+            nc.vector.scalar_tensor_tensor(part[:], h2[t][:, 0:S], 2.0, sg[:], ALU.mult, ALU.mult)
+            for cols in [halves[0], slice(256, 384), slice(384, 512)] if t == last else [whole]:
                 nc.scalar.activation(
                     sg2[:, cols],
-                    mb[t][:].indirect(n4_t[:, cols.start // 16 : cols.stop // 16]),
+                    h2[t][:].indirect(entries(n4_t, cols)),
                     ACT.Sigmoid,
                     bias=bias2[:, col],
                     scale=minus[:, 1, col],

from contextlib import ExitStack

import concourse.mybir as mybir

K, T, S, G, H, W = 512, 1024, 512, 2048, 512, 1024
FLOPS = 2 * K * H * S * 2

F32 = mybir.dt.float32
BF16 = mybir.dt.bfloat16
I32 = mybir.dt.int32
U32 = mybir.dt.uint32
U16 = mybir.dt.uint16
U8 = mybir.dt.uint8
FP8X4 = mybir.dt.float8_e4m3fn_x4
ALU = mybir.AluOpType
ACT = mybir.ActivationFunctionType

P = 128
PACK = 4
SPARE = 32


def tile_picked_codeghopmecr_none_p_kernel(
    tc, x_words, x_scales, d_words, d_scales, gs, sl, th, sl2, th2, offs, k1, n1, n2, k2, n3, n4, out
):
    nc = tc.nc
    with ExitStack() as ctx:
        sb = ctx.enter_context(tc.tile_pool(name="sb", bufs=1))
        psum = ctx.enter_context(tc.psum_pool(name="psum", bufs=1))

        def load_list(name, src):
            tile = sb.tile(list(src.shape), U16, name=name)
            nc.sync.dma_start(tile[:], src)
            return tile

        def cleared(name, width):
            tile = sb.tile([P, width], U8, name=name, align_bytes=64)
            nc.vector.memset(tile[:].bitcast(I32), 0)
            return tile

        def load_words(name, src, width, queue):
            tile = sb.tile([P, width], U32, name=name, align_bytes=64)
            queue.dma_start(tile[:].bitcast(I32), src[0].rearrange("p n t -> p (n t)").bitcast(I32))
            return tile

        def load_vec(name, src):
            tile = sb.tile([P, PACK], F32, name=name)
            nc.sync.dma_start(tile[:], src.rearrange("(p t) o -> p (t o)", t=PACK))
            return tile

        halves = [slice(0, S // 2), slice(S // 2, S)]
        whole = slice(0, S)

        def entries(offsets, cols):
            return offsets[:, cols.start // 16 : cols.stop // 16]

        def pick_and_deal(name, dtype, table, offsets, tag, pieces):
            run = 16 if dtype == U8 else 4
            picked = sb.tile([P, H], dtype, name=name + "_picked", tag=tag, align_bytes=64)
            dealt = sb.tile([P, H], dtype, name=name, align_bytes=64)
            for cols in pieces:
                nc.vector.tensor_copy(picked[:, cols], table[:].indirect(entries(offsets, cols)))
            for cols in pieces:
                nc.vector.tensor_copy(
                    dealt[:]
                    .rearrange("p (t m) -> p t m", t=PACK)[:, :, cols.start // PACK : cols.stop // PACK]
                    .rearrange("p t (c i) -> p c t i", i=run),
                    picked[:, cols].rearrange("p (c i t) -> p c t i", t=PACK, i=run),
                )
            return dealt

        def place_odd_rows(plane, queue):
            words = plane[:].bitcast(I32)
            for r in range(1, 4):
                queue.dma_start(words[r:P:32, :], words[8 * r : P : 32, :])

        d_sc = cleared("d_sc", G)
        x_sc = cleared("x_sc", T)
        k1_t = load_list("k1_t", k1)
        offs_t = load_list("offs_t", offs)
        nc.sync.dma_start(d_sc[:].bitcast(I32)[0:P:8, :], d_scales[0].bitcast(I32))
        for q in range(4):
            nc.sync.dma_start(
                x_sc[:].bitcast(I32)[32 * q : 32 * q + 4, :], x_scales[0].bitcast(I32)[4 * q : 4 * q + 4, :]
            )
        d_w = load_words("d_w", d_words, G, nc.sync)
        x_w = load_words("x_w", x_words, T, nc.sync)

        plane1 = pick_and_deal("plane1", U8, d_sc, k1_t, "d1_sc", halves)
        place_odd_rows(plane1, nc.sync)
        xg_sc = sb.tile([P, S], U8, name="xg_sc", align_bytes=64)
        nc.vector.tensor_copy(xg_sc[:], x_sc[:].indirect(offs_t[:]))
        w1 = pick_and_deal("w1", U32, d_w, k1_t, "d1_w", halves)
        xg_w = sb.tile([P, S], U32, name="xg_w", align_bytes=64)
        for cols in halves:
            nc.vector.tensor_copy(xg_w[:, cols], x_w[:].indirect(offs_t[:, cols.start // 16 : cols.stop // 16]))

        k2_t = load_list("k2_t", k2)
        n1_t = load_list("n1_t", n1)
        n2_t = load_list("n2_t", n2)
        n3_t = load_list("n3_t", n3)
        n4_t = load_list("n4_t", n4)
        slopes = sb.tile([P, 2, 2 * PACK], F32, name="slopes")
        for i, src in enumerate((sl, sl2)):
            nc.sync.dma_start(slopes[:, i, 0:PACK], src.rearrange("(p t) o -> p (t o)", t=PACK))
        th_t = load_vec("th_t", th)
        th2_t = load_vec("th2_t", th2)
        gs_t = load_vec("gs_t", gs)

        minus = sb.tile([P, 2, PACK], F32, name="minus")
        bias1 = sb.tile([P, PACK], F32, name="bias1")
        bias2 = sb.tile([P, PACK], F32, name="bias2")
        gain = sb.tile([P, PACK], F32, name="gain")
        nc.scalar.activation(minus[:], slopes[:, :, 0:PACK], ACT.Copy, scale=-1.0)
        nc.gpsimd.tensor_tensor(bias1[:], minus[:, 0, :], th_t[:], ALU.mult)
        nc.gpsimd.tensor_tensor(bias2[:], slopes[:, 1, 0:PACK], th2_t[:], ALU.mult)
        nc.gpsimd.tensor_scalar(gain[:], gs_t[:], 0.0625, 0.0, ALU.mult, ALU.add)

        banks = [psum.tile([P, S], F32, name="bank%d" % b) for b in range(2 * PACK)]
        h = [sb.tile([P, S + SPARE], F32, name="h%d" % t) for t in range(PACK)]
        early = [(0, halves[0], PACK), (1, halves[0], PACK + 1)]
        late = [(0, halves[1], 0), (1, halves[1], 1), (2, whole, 2), (3, whole, 3)]
        for t, cols, bank in early + late:
            rows = slice(t * P, (t + 1) * P)
            nc.tensor.matmul_mx(
                out=banks[bank][:, cols],
                lhsT=w1[:, rows].bitcast(FP8X4),
                lhsT_scale=plane1[:, rows],
                rhs=xg_w[:, cols].bitcast(FP8X4),
                rhs_scale=xg_sc[:, cols],
                start=True,
                stop=True,
            )

        def evac(piece):
            t, cols, bank = piece
            nc.scalar.activation(h[t][:, cols], banks[bank][:, cols], ACT.Copy)

        for piece in early:
            evac(piece)

        plane2 = pick_and_deal("plane2", U8, d_sc, k2_t, "d2_sc", halves)
        place_odd_rows(plane2, nc.sync)

        mb = [sb.tile([P, W], F32, name="mb%d" % t) for t in range(PACK)]
        st = [sb.tile([P, S + SPARE], F32, name="st%d" % t) for t in range(PACK)]
        mx = [sb.tile([P, S], F32, name="mx%d" % t, tag="mx%d" % t, align_bytes=64) for t in range(PACK)]
        stn = [sb.tile([P, S], F32, name="stn%d" % t) for t in range(PACK)]
        big = [sb.tile([P, S], F32, name="big%d" % t) for t in range(PACK)]
        zpair = sb.tile([P, 2, 2, S // 2, 2], BF16, name="zpair", align_bytes=64)
        z = sb.tile([P, S * PACK], BF16, name="z", align_bytes=64)

        def members(t, half, on_vector):
            window = h[t][:].indirect(n1_t[:, half * 32 : (half + 1) * 32])
            dst = mb[t][:, half * S : (half + 1) * S]
            if on_vector:
                nc.vector.tensor_copy(dst, window)
            else:
                nc.scalar.activation(dst, window, ACT.Copy)

        def stand(t):
            pairs = mb[t][:].rearrange("p (j e) -> p e j", e=2)
            nc.vector.tensor_tensor(mx[t][:], pairs[:, 0, :], pairs[:, 1, :], ALU.max)
            nc.vector.tensor_tensor(st[t][:, 0:S], h[t][:, 0:S], mx[t][:], ALU.subtract)

        def neighbour(t, cols, on_vector):
            window = st[t][:].indirect(n2_t[:, cols.start // 16 : cols.stop // 16])
            if on_vector:
                nc.vector.tensor_copy(stn[t][:, cols], window)
            else:
                nc.scalar.activation(stn[t][:, cols], window, ACT.Copy)

        def weigh(t, cols):
            nc.vector.tensor_tensor(big[t][:, cols], st[t][:, cols], stn[t][:, cols], ALU.max)
            nc.vector.tensor_scalar(
                zpair[:, 2 * cols.start // S : 2 * cols.stop // S, t // 2, :, t % 2],
                big[t][:, cols].rearrange("p (a j) -> p a j", j=S // 2),
                gain[:, t : t + 1],
                None,
                ALU.mult,
            )

        z_w = sb.tile([P, S], U32, name="z_w", align_bytes=64)
        z_sc = sb.tile([P, S], U8, name="z_sc", align_bytes=64)
        z_words = z[:].bitcast(F32).rearrange("p (j u) -> p j u", u=2)

        def quantise(cols):
            pair_words = zpair[:, 2 * cols.start // S].rearrange("p u j e -> p u (j e)").bitcast(F32)
            nc.vector.tensor_copy(z_words[:, cols, :], pair_words.rearrange("p u j -> p j u"))
            nc.vector.quantize_mx(
                out=z_w[:, cols].bitcast(FP8X4), scales=z_sc[:, cols], in_=z[:, PACK * cols.start : PACK * cols.stop]
            )

        evac(late[0])
        members(0, 0, False)
        members(0, 1, True)
        evac(late[1])
        stand(0)
        members(1, 0, False)
        members(1, 1, True)
        evac(late[2])
        stand(1)
        members(2, 0, False)
        members(2, 1, False)
        w2 = pick_and_deal("w2", U32, d_w, k2_t, "mx0", [whole])
        evac(late[3])
        stand(2)
        members(3, 0, False)
        members(3, 1, False)
        stand(3)
        neighbour(0, halves[0], True)
        neighbour(0, halves[1], False)
        weigh(0, whole)
        neighbour(1, whole, False)
        neighbour(2, whole, False)
        for cols in halves:
            neighbour(3, cols, False)
        weigh(1, whole)
        weigh(2, whole)
        for cols in halves:
            weigh(3, cols)
            quantise(cols)

        out_rows = out.rearrange("(p t) c -> p t c", t=PACK)
        pieces = [(0, halves[0], PACK), (0, halves[1], 0)] + [(t, whole, PACK + t) for t in range(1, PACK)]
        for t, cols, bank in pieces:
            rows = slice(t * P, (t + 1) * P)
            nc.tensor.matmul_mx(
                out=banks[bank][:, cols],
                lhsT=w2[:, rows].bitcast(FP8X4),
                lhsT_scale=plane2[:, rows],
                rhs=z_w[:, cols].bitcast(FP8X4),
                rhs_scale=z_sc[:, cols],
                start=True,
                stop=True,
            )
        last = PACK - 1
        h2 = mb[:last] + [mx[last]]
        for t, cols, bank in pieces:
            nc.vector.tensor_scalar(h2[t][:, cols], banks[bank][:, cols], 0.0625, None, ALU.mult)
        for t in range(PACK):
            col = slice(t, t + 1)
            sg = sb.tile([P, S], F32, name="sg%d" % t)
            sg2 = sb.tile([P, S], F32, name="sg2_%d" % t)
            part = sb.tile([P, S], F32, name="part%d" % t, tag="part")
            res = sb.tile([P, S], F32, name="res%d" % t)
            for cols in halves if t == last else [whole]:
                nc.scalar.activation(
                    sg[:, cols],
                    h2[t][:].indirect(entries(n3_t, cols)),
                    ACT.Sigmoid,
                    bias=bias1[:, col],
                    scale=slopes[:, 0, col],
                )
            nc.vector.scalar_tensor_tensor(part[:], h2[t][:, 0:S], 2.0, sg[:], ALU.mult, ALU.mult)
            for cols in [halves[0], slice(256, 384), slice(384, 512)] if t == last else [whole]:
                nc.scalar.activation(
                    sg2[:, cols],
                    h2[t][:].indirect(entries(n4_t, cols)),
                    ACT.Sigmoid,
                    bias=bias2[:, col],
                    scale=minus[:, 1, col],
                )
                nc.vector.tensor_tensor(res[:, cols], part[:, cols], sg2[:, cols], ALU.mult)
                nc.sync.dma_start(out_rows[:, t, cols], res[:, cols])
